import numpy as np, ml_dtypes
CORES = [2,34,66,98,130,162,194,226,258,290,322,354,386,418,450,482]
N = 16
WB, KB, QP = 3, 1, 128
WID = [16,64,16,128,112,48,32,80,128,48,96,64,64,80,80,128]
def setup_inputs(rng):
    return {"q": rng.standard_normal((N, 128, QP), dtype=np.float32).astype(ml_dtypes.bfloat16), "k": rng.standard_normal((N, 128, KB * 128), dtype=np.float32).astype(ml_dtypes.bfloat16), "v": rng.standard_normal((N, 128, KB * 128), dtype=np.float32).astype(ml_dtypes.bfloat16)}
def setup_inputs_big(rng):
    d = setup_inputs(rng)
    for k in ("q", "k", "v"): d[k] = (d[k].astype(np.float32) * 1024.0).astype(d[k].dtype)
    return d
def setup_inputs_small(rng):
    d = setup_inputs(rng)
    for k in ("q", "k", "v"): d[k] = (d[k].astype(np.float32) * (1 / 1024.0)).astype(d[k].dtype)
    return d
def setup_inputs_apart(rng):
    d = setup_inputs(rng)
    f = (10.0 ** rng.permutation(np.linspace(-1.5, 1.5, N))).astype(np.float32).reshape(N, 1, 1)
    for k in ("q", "k", "v"): d[k] = (d[k].astype(np.float32) * f).astype(d[k].dtype)
    return d
def whole(q, k, v):
    Q, K, V = q.astype(np.float64), k.astype(np.float64), v.astype(np.float64)
    y = np.zeros((N, 128, QP))
    for r in range(N):
        for j in range(max(0, r - WB), r + 1):
            for b in range(KB):
                S = np.maximum(K[j][:, 128 * b:128 * b + 128].T @ Q[r], 0.0)
                y[r] += V[j][:, 128 * b:128 * b + 128].T @ S
    return {"y": y.astype(ml_dtypes.bfloat16 if q.dtype != np.float64 else np.float64)}
def reference(q, k, v):
    o = whole(q, k, v)["y"].copy()
    for r in range(N):
        o[r][:, WID[r]:] = np.nan
    return {"y": o}

@@ -1,0 +1,107 @@
+from concourse.bass import DstId, RemoteDMATransfer
+from concourse.mybir import dt, AluOpType
+
+WB = 3
+NSLOT = WB + 1
+NE = 8
+
+SCRATCH = {
+    "qs": ("sbuf", [128, 128], "bfloat16"),
+    "zero": ("sbuf", [128, 128], "float32"),
+    "ysb": ("sbuf", [128, 128], "bfloat16"),
+    "pO": ("psum", [128, 512], "float32"),
+}
+for _i in range(NSLOT):
+    SCRATCH["kv%d" % _i] = ("sbuf", [128, 256], "bfloat16")
+    SCRATCH["s%d" % _i] = ("sbuf", [128, 128], "bfloat16")
+    SCRATCH["pS%d" % _i] = ("psum", [128, 512], "float32")
+
+SEMAPHORES = ["ld", "ldq", "zf", "sent", "sO", "sY", "st"] + \
+    ["arr%d" % _i for _i in range(NSLOT)] + ["sS%d" % _i for _i in range(NSLOT)] + ["sR%d" % _i for _i in range(NSLOT)]
+
+
+def _pick(mask, n):
+    out, b = 0, 1
+    while n and b <= mask:
+        if mask & b:
+            out |= b
+            n -= 1
+        b <<= 1
+    return out
+
+
+def rank_program(g, core, T, topo):
+    r = T.rank_of(core)
+    if r is None:
+        return
+    cores = T.cores
+    n = len(cores)
+    w = T.tables["WID"][r]
+
+    def crosses(a, b):
+        return topo.rack(topo.host(cores[a])) != topo.rack(topo.host(cores[b]))
+
+    def dests(j):
+        return sorted(range(j + 1, min(n, j + WB + 1)), key=lambda x: (not crosses(j, x), x))
+
+    own = T["kv%d" % (r % NSLOT)]
+    g.sync.dma_start(own[:, 0:128], T.k[:, :]).then_inc(T.sem.ld, 16)
+    g.scalar.dma_start(own[:, 128:256], T.v[:, :]).then_inc(T.sem.ld, 16)
+    g.sync.dma_start(T.qs[:, 0:w], T.q[:, 0:w]).then_inc(T.sem.ldq, 16)
+    g.vector.memset(T.zero[:, 0:w], 0.0).then_inc(T.sem.zf, 1)
+
+    ds = dests(r)
+    if ds:
+        m = topo.mask(core, cores[ds[0]])
+        for d in ds:
+            m &= topo.mask(core, cores[d])
+        m = _pick(m, NE)
+        ids = []
+        for d in ds:
+            rid, pid = topo.addr(cores[d], core)
+            ids.append(DstId(rid=rid, pnc=pid))
+        g.wait_ge(T.sem.ld, 32)
+        g.remote_dma_fused([RemoteDMATransfer(dst_ids=ids, dma_engine_mask=m, remote_sem=T.sem["arr%d" % (r % NSLOT)],
+                                              srcs=[own[:]], dsts=[own[:] for _ in ds])], local_sem=T.sem.sent)
+
+    srcs = sorted(range(max(0, r - WB), r), key=lambda j: (dests(j).index(r), crosses(j, r), -j))
+    blocks = [r] + srcs
+    last = len(blocks) - 1
+
+    def s_mm(j):
+        i = j % NSLOT
+        if j == r:
+            g.tensor.wait_ge(T.sem.ld, 32)
+            g.tensor.wait_ge(T.sem.ldq, 16)
+        else:
+            g.tensor.wait_ge(T.sem["arr%d" % i], NE)
+        g.tensor.matmul(T["pS%d" % i][:, 0:w], T["kv%d" % i][:, 0:128], T.qs[:, 0:w], start=True, stop=True) \
+            .then_inc(T.sem["sS%d" % i], 1)
+
+    def o_mm(pos):
+        i = blocks[pos] % NSLOT
+        g.tensor.wait_ge(T.sem["sR%d" % i], 1)
+        mm = g.tensor.matmul(T.pO[:, 0:w], T["kv%d" % i][:, 128:256], T["s%d" % i][:, 0:w], start=(pos == 0), stop=(pos == last))
+        if pos == last:
+            mm.then_inc(T.sem.sO, 1)
+
+    s_mm(blocks[0])
+    for pos in range(1, last + 1):
+        s_mm(blocks[pos])
+        o_mm(pos - 1)
+    o_mm(last)
+
+    g.vector.wait_ge(T.sem.zf, 1)
+    for j in blocks:
+        i = j % NSLOT
+        g.vector.wait_ge(T.sem["sS%d" % i], 1)
+        g.vector.tensor_tensor(T["s%d" % i][:, 0:w], T["pS%d" % i][:, 0:w], T.zero[:, 0:w], AluOpType.max) \
+            .then_inc(T.sem["sR%d" % i], 1)
+    g.vector.wait_ge(T.sem.sO, 1)
+    g.vector.tensor_copy(T.ysb[:, 0:w], T.pO[:, 0:w]).then_inc(T.sem.sY, 1)
+
+    g.sync.wait_ge(T.sem.sY, 1)
+    g.sync.dma_start(T.y[:, 0:w], T.ysb[:, 0:w]).then_inc(T.sem.st, 16)
+    g.sync.wait_ge(T.sem.st, 16)
+    if ds:
+        g.wait_ge(T.sem.sent, NE)

@@ -3,7 +3,8 @@ from concourse.mybir import dt, AluOpType
 
 WB = 3
 NSLOT = WB + 1
-NE = 8
+MAINC = 64
+HELPC = (256 - MAINC) // 3
 
 SCRATCH = {
     "qs": ("sbuf", [128, 128], "bfloat16"),
@@ -16,27 +17,21 @@ for _i in range(NSLOT):
     SCRATCH["s%d" % _i] = ("sbuf", [128, 128], "bfloat16")
     SCRATCH["pS%d" % _i] = ("psum", [128, 512], "float32")
 
-SEMAPHORES = ["ld", "ldq", "zf", "sent", "sO", "sY", "st"] + \
+SEMAPHORES = ["ld", "ldq", "zf", "sent", "hin", "sO", "sY", "st"] + \
     ["arr%d" % _i for _i in range(NSLOT)] + ["sS%d" % _i for _i in range(NSLOT)] + ["sR%d" % _i for _i in range(NSLOT)]
 
 
-def _pick(mask, n):
-    out, b = 0, 1
-    while n and b <= mask:
-        if mask & b:
-            out |= b
-            n -= 1
-        b <<= 1
-    return out
+def _bits(mask):
+    return [b for b in range(mask.bit_length()) if (mask >> b) & 1]
+
+
+def _count(mask):
+    return len(_bits(mask))
 
 
 def rank_program(g, core, T, topo):
-    r = T.rank_of(core)
-    if r is None:
-        return
     cores = T.cores
     n = len(cores)
-    w = T.tables["WID"][r]
 
     def crosses(a, b):
         return topo.rack(topo.host(cores[a])) != topo.rack(topo.host(cores[b]))
@@ -44,25 +39,76 @@ def rank_program(g, core, T, topo):
     def dests(j):
         return sorted(range(j + 1, min(n, j + WB + 1)), key=lambda x: (not crosses(j, x), x))
 
+    def helpers(j):
+        c = cores[j]
+        chipc = [x for x in range(c - 8, c + 9) if x >= 0 and x != c and topo.host(x) == topo.host(c) and topo.chip(x) == topo.chip(c)]
+        mine = [x for x in chipc if topo.die(x) == topo.die(c)]
+        other = [x for x in chipc if topo.die(x) != topo.die(c)]
+        return [max(mine, key=lambda x: abs(x - c)), other[0], other[-1]]
+
+    def piece(p):
+        if p == 0:
+            return 0, MAINC
+        return MAINC + (p - 1) * HELPC, MAINC + p * HELPC
+
+    def off_mask(src, ds):
+        m = topo.mask(src, cores[ds[0]])
+        for d in ds:
+            m &= topo.mask(src, cores[d])
+        return m
+
+    def send_piece(j, p):
+        ds = dests(j)
+        lo, hi = piece(p)
+        buf = T["kv%d" % (j % NSLOT)]
+        ids = []
+        for d in ds:
+            rid, pid = topo.addr(cores[d], core)
+            ids.append(DstId(rid=rid, pnc=pid))
+        m = off_mask(core, ds)
+        g.remote_dma_fused([RemoteDMATransfer(dst_ids=ids, dma_engine_mask=m, remote_sem=T.sem["arr%d" % (j % NSLOT)],
+                                              srcs=[buf[:, lo:hi]], dsts=[buf[:, lo:hi] for _ in ds])], local_sem=T.sem.sent)
+        return _count(m)
+
+    def hand_masks(j):
+        c = cores[j]
+        out = []
+        for p, h in enumerate(helpers(j)):
+            b = _bits(topo.mask(c, h))
+            b = b[len(b) - 4 * (p + 1):len(b) - 4 * p]
+            out.append(sum(1 << x for x in b))
+        return out
+
+    r = T.rank_of(core)
+    if r is None:
+        for j in range(n):
+            if dests(j) and core in helpers(j):
+                p = helpers(j).index(core)
+                g.wait_ge(T.sem.hin, _count(hand_masks(j)[p]))
+                ne = send_piece(j, p + 1)
+                g.wait_ge(T.sem.sent, ne)
+        return
+
+    w = T.tables["WID"][r]
     own = T["kv%d" % (r % NSLOT)]
     g.sync.dma_start(own[:, 0:128], T.k[:, :]).then_inc(T.sem.ld, 16)
     g.scalar.dma_start(own[:, 128:256], T.v[:, :]).then_inc(T.sem.ld, 16)
     g.sync.dma_start(T.qs[:, 0:w], T.q[:, 0:w]).then_inc(T.sem.ldq, 16)
     g.vector.memset(T.zero[:, 0:w], 0.0).then_inc(T.sem.zf, 1)
 
-    ds = dests(r)
-    if ds:
-        m = topo.mask(core, cores[ds[0]])
-        for d in ds:
-            m &= topo.mask(core, cores[d])
-        m = _pick(m, NE)
-        ids = []
-        for d in ds:
-            rid, pid = topo.addr(cores[d], core)
-            ids.append(DstId(rid=rid, pnc=pid))
+    nsent = 0
+    if dests(r):
         g.wait_ge(T.sem.ld, 32)
-        g.remote_dma_fused([RemoteDMATransfer(dst_ids=ids, dma_engine_mask=m, remote_sem=T.sem["arr%d" % (r % NSLOT)],
-                                              srcs=[own[:]], dsts=[own[:] for _ in ds])], local_sem=T.sem.sent)
+        trs = []
+        for p, h in enumerate(helpers(r)):
+            lo, hi = piece(p + 1)
+            rid, pid = topo.addr(h, core)
+            m = hand_masks(r)[p]
+            trs.append(RemoteDMATransfer(dst_ids=[DstId(rid=rid, pnc=pid)], dma_engine_mask=m, remote_sem=T.sem.hin,
+                                         srcs=[own[:, lo:hi]], dsts=[own[:, lo:hi]]))
+            nsent += _count(m)
+        g.remote_dma_fused(trs, local_sem=T.sem.sent)
+        nsent += send_piece(r, 0)
 
     srcs = sorted(range(max(0, r - WB), r), key=lambda j: (dests(j).index(r), crosses(j, r), -j))
     blocks = [r] + srcs
@@ -74,7 +120,8 @@ def rank_program(g, core, T, topo):
             g.tensor.wait_ge(T.sem.ld, 32)
             g.tensor.wait_ge(T.sem.ldq, 16)
         else:
-            g.tensor.wait_ge(T.sem["arr%d" % i], NE)
+            tot = sum(_count(off_mask(c, dests(j))) for c in [cores[j]] + helpers(j))
+            g.tensor.wait_ge(T.sem["arr%d" % i], tot)
         g.tensor.matmul(T["pS%d" % i][:, 0:w], T["kv%d" % i][:, 0:128], T.qs[:, 0:w], start=True, stop=True) \
             .then_inc(T.sem["sS%d" % i], 1)
 
@@ -103,5 +150,5 @@ def rank_program(g, core, T, topo):
     g.sync.wait_ge(T.sem.sY, 1)
     g.sync.dma_start(T.y[:, 0:w], T.ysb[:, 0:w]).then_inc(T.sem.st, 16)
     g.sync.wait_ge(T.sem.st, 16)
-    if ds:
-        g.wait_ge(T.sem.sent, NE)
+    if nsent:
+        g.wait_ge(T.sem.sent, nsent)

@@ -3,7 +3,7 @@ from concourse.mybir import dt, AluOpType
 
 WB = 3
 NSLOT = WB + 1
-MAINC = 64
+MAINC = 100
 HELPC = (256 - MAINC) // 3
 
 SCRATCH = {
@@ -33,11 +33,8 @@ def rank_program(g, core, T, topo):
     cores = T.cores
     n = len(cores)
 
-    def crosses(a, b):
-        return topo.rack(topo.host(cores[a])) != topo.rack(topo.host(cores[b]))
-
     def dests(j):
-        return sorted(range(j + 1, min(n, j + WB + 1)), key=lambda x: (not crosses(j, x), x))
+        return list(range(j + 1, min(n, j + WB + 1)))
 
     def helpers(j):
         c = cores[j]
@@ -110,8 +107,7 @@ def rank_program(g, core, T, topo):
         g.remote_dma_fused(trs, local_sem=T.sem.sent)
         nsent += send_piece(r, 0)
 
-    srcs = sorted(range(max(0, r - WB), r), key=lambda j: (dests(j).index(r), crosses(j, r), -j))
-    blocks = [r] + srcs
+    blocks = [r] + list(range(r - 1, max(0, r - WB) - 1, -1))
     last = len(blocks) - 1
 
     def s_mm(j):

@@ -3,8 +3,8 @@ from concourse.mybir import dt, AluOpType
 
 WB = 3
 NSLOT = WB + 1
-MAINC = 100
-HELPC = (256 - MAINC) // 3
+MAINC = 50
+HELPC = (128 - MAINC) // 3
 
 SCRATCH = {
     "qs": ("sbuf", [128, 128], "bfloat16"),
@@ -17,8 +17,9 @@ for _i in range(NSLOT):
     SCRATCH["s%d" % _i] = ("sbuf", [128, 128], "bfloat16")
     SCRATCH["pS%d" % _i] = ("psum", [128, 512], "float32")
 
-SEMAPHORES = ["ld", "ldq", "zf", "sent", "hin", "sO", "sY", "st"] + \
-    ["arr%d" % _i for _i in range(NSLOT)] + ["sS%d" % _i for _i in range(NSLOT)] + ["sR%d" % _i for _i in range(NSLOT)]
+SEMAPHORES = ["ldk", "ldv", "ldq", "zf", "sent", "hink", "hinv", "sO", "sY", "st"] + \
+    ["ak%d" % _i for _i in range(NSLOT)] + ["av%d" % _i for _i in range(NSLOT)] + \
+    ["sS%d" % _i for _i in range(NSLOT)] + ["sR%d" % _i for _i in range(NSLOT)]
 
 
 def _bits(mask):
@@ -43,10 +44,11 @@ def rank_program(g, core, T, topo):
         other = [x for x in chipc if topo.die(x) != topo.die(c)]
         return [max(mine, key=lambda x: abs(x - c)), other[0], other[-1]]
 
-    def piece(p):
+    def piece(p, half):
+        base = 128 * half
         if p == 0:
-            return 0, MAINC
-        return MAINC + (p - 1) * HELPC, MAINC + p * HELPC
+            return base, base + MAINC
+        return base + MAINC + (p - 1) * HELPC, base + MAINC + p * HELPC
 
     def off_mask(src, ds):
         m = topo.mask(src, cores[ds[0]])
@@ -54,16 +56,17 @@ def rank_program(g, core, T, topo):
             m &= topo.mask(src, cores[d])
         return m
 
-    def send_piece(j, p):
+    def send_piece(j, p, half):
         ds = dests(j)
-        lo, hi = piece(p)
+        lo, hi = piece(p, half)
         buf = T["kv%d" % (j % NSLOT)]
         ids = []
         for d in ds:
             rid, pid = topo.addr(cores[d], core)
             ids.append(DstId(rid=rid, pnc=pid))
         m = off_mask(core, ds)
-        g.remote_dma_fused([RemoteDMATransfer(dst_ids=ids, dma_engine_mask=m, remote_sem=T.sem["arr%d" % (j % NSLOT)],
+        sem = T.sem[("av%d" if half else "ak%d") % (j % NSLOT)]
+        g.remote_dma_fused([RemoteDMATransfer(dst_ids=ids, dma_engine_mask=m, remote_sem=sem,
                                               srcs=[buf[:, lo:hi]], dsts=[buf[:, lo:hi] for _ in ds])], local_sem=T.sem.sent)
         return _count(m)
 
@@ -81,58 +84,71 @@ def rank_program(g, core, T, topo):
         for j in range(n):
             if dests(j) and core in helpers(j):
                 p = helpers(j).index(core)
-                g.wait_ge(T.sem.hin, _count(hand_masks(j)[p]))
-                ne = send_piece(j, p + 1)
+                ne = 0
+                g.wait_ge(T.sem.hink, _count(hand_masks(j)[p]))
+                ne += send_piece(j, p + 1, 0)
+                g.wait_ge(T.sem.hinv, _count(hand_masks(j)[p]))
+                ne += send_piece(j, p + 1, 1)
                 g.wait_ge(T.sem.sent, ne)
         return
 
     w = T.tables["WID"][r]
     own = T["kv%d" % (r % NSLOT)]
-    g.sync.dma_start(own[:, 0:128], T.k[:, :]).then_inc(T.sem.ld, 16)
-    g.scalar.dma_start(own[:, 128:256], T.v[:, :]).then_inc(T.sem.ld, 16)
+    g.sync.dma_start(own[:, 0:128], T.k[:, :]).then_inc(T.sem.ldk, 16)
+    g.scalar.dma_start(own[:, 128:256], T.v[:, :]).then_inc(T.sem.ldv, 16)
     g.sync.dma_start(T.qs[:, 0:w], T.q[:, 0:w]).then_inc(T.sem.ldq, 16)
     g.vector.memset(T.zero[:, 0:w], 0.0).then_inc(T.sem.zf, 1)
 
     nsent = 0
     if dests(r):
-        g.wait_ge(T.sem.ld, 32)
-        trs = []
-        for p, h in enumerate(helpers(r)):
-            lo, hi = piece(p + 1)
-            rid, pid = topo.addr(h, core)
-            m = hand_masks(r)[p]
-            trs.append(RemoteDMATransfer(dst_ids=[DstId(rid=rid, pnc=pid)], dma_engine_mask=m, remote_sem=T.sem.hin,
-                                         srcs=[own[:, lo:hi]], dsts=[own[:, lo:hi]]))
-            nsent += _count(m)
-        g.remote_dma_fused(trs, local_sem=T.sem.sent)
-        nsent += send_piece(r, 0)
+        for half in (0, 1):
+            g.wait_ge(T.sem.ldv if half else T.sem.ldk, 16)
+            trs = []
+            for p, h in enumerate(helpers(r)):
+                lo, hi = piece(p + 1, half)
+                rid, pid = topo.addr(h, core)
+                m = hand_masks(r)[p]
+                trs.append(RemoteDMATransfer(dst_ids=[DstId(rid=rid, pnc=pid)], dma_engine_mask=m,
+                                             remote_sem=T.sem.hinv if half else T.sem.hink,
+                                             srcs=[own[:, lo:hi]], dsts=[own[:, lo:hi]]))
+                nsent += _count(m)
+            g.remote_dma_fused(trs, local_sem=T.sem.sent)
+            nsent += send_piece(r, 0, half)
 
     blocks = [r] + list(range(r - 1, max(0, r - WB) - 1, -1))
     last = len(blocks) - 1
 
+    def arrivals(j):
+        return sum(_count(off_mask(c, dests(j))) for c in [cores[j]] + helpers(j))
+
     def s_mm(j):
         i = j % NSLOT
         if j == r:
-            g.tensor.wait_ge(T.sem.ld, 32)
+            g.tensor.wait_ge(T.sem.ldk, 16)
             g.tensor.wait_ge(T.sem.ldq, 16)
         else:
-            tot = sum(_count(off_mask(c, dests(j))) for c in [cores[j]] + helpers(j))
-            g.tensor.wait_ge(T.sem["arr%d" % i], tot)
+            g.tensor.wait_ge(T.sem["ak%d" % i], arrivals(j))
         g.tensor.matmul(T["pS%d" % i][:, 0:w], T["kv%d" % i][:, 0:128], T.qs[:, 0:w], start=True, stop=True) \
             .then_inc(T.sem["sS%d" % i], 1)
 
     def o_mm(pos):
-        i = blocks[pos] % NSLOT
+        j = blocks[pos]
+        i = j % NSLOT
         g.tensor.wait_ge(T.sem["sR%d" % i], 1)
+        if j == r:
+            g.tensor.wait_ge(T.sem.ldv, 16)
+        else:
+            g.tensor.wait_ge(T.sem["av%d" % i], arrivals(j))
         mm = g.tensor.matmul(T.pO[:, 0:w], T["kv%d" % i][:, 128:256], T["s%d" % i][:, 0:w], start=(pos == 0), stop=(pos == last))
         if pos == last:
             mm.then_inc(T.sem.sO, 1)
 
     s_mm(blocks[0])
+    o_mm(0)
     for pos in range(1, last + 1):
         s_mm(blocks[pos])
-        o_mm(pos - 1)
-    o_mm(last)
+    for pos in range(1, last + 1):
+        o_mm(pos)
 
     g.vector.wait_ge(T.sem.zf, 1)
     for j in blocks:

from concourse.bass import DstId, RemoteDMATransfer
from concourse.mybir import dt, AluOpType

WB = 3
NSLOT = WB + 1
MAINC = 50
HELPC = (128 - MAINC) // 3

SCRATCH = {
    "qs": ("sbuf", [128, 128], "bfloat16"),
    "zero": ("sbuf", [128, 128], "float32"),
    "ysb": ("sbuf", [128, 128], "bfloat16"),
    "pO": ("psum", [128, 512], "float32"),
}
for _i in range(NSLOT):
    SCRATCH["kv%d" % _i] = ("sbuf", [128, 256], "bfloat16")
    SCRATCH["s%d" % _i] = ("sbuf", [128, 128], "bfloat16")
    SCRATCH["pS%d" % _i] = ("psum", [128, 512], "float32")

SEMAPHORES = ["ldk", "ldv", "ldq", "zf", "sent", "hink", "hinv", "sO", "sY", "st"] + \
    ["ak%d" % _i for _i in range(NSLOT)] + ["av%d" % _i for _i in range(NSLOT)] + \
    ["sS%d" % _i for _i in range(NSLOT)] + ["sR%d" % _i for _i in range(NSLOT)]


def _bits(mask):
    return [b for b in range(mask.bit_length()) if (mask >> b) & 1]


def _count(mask):
    return len(_bits(mask))


def rank_program(g, core, T, topo):
    cores = T.cores
    n = len(cores)

    def dests(j):
        return list(range(j + 1, min(n, j + WB + 1)))

    def helpers(j):
        c = cores[j]
        chipc = [x for x in range(c - 8, c + 9) if x >= 0 and x != c and topo.host(x) == topo.host(c) and topo.chip(x) == topo.chip(c)]
        mine = [x for x in chipc if topo.die(x) == topo.die(c)]
        other = [x for x in chipc if topo.die(x) != topo.die(c)]
        return [max(mine, key=lambda x: abs(x - c)), other[0], other[-1]]

    def piece(p, half):
        base = 128 * half
        if p == 0:
            return base, base + MAINC
        return base + MAINC + (p - 1) * HELPC, base + MAINC + p * HELPC

    def off_mask(src, ds):
        m = topo.mask(src, cores[ds[0]])
        for d in ds:
            m &= topo.mask(src, cores[d])
        return m

    def send_piece(j, p, half):
        ds = dests(j)
        lo, hi = piece(p, half)
        buf = T["kv%d" % (j % NSLOT)]
        ids = []
        for d in ds:
            rid, pid = topo.addr(cores[d], core)
            ids.append(DstId(rid=rid, pnc=pid))
        m = off_mask(core, ds)
        sem = T.sem[("av%d" if half else "ak%d") % (j % NSLOT)]
        g.remote_dma_fused([RemoteDMATransfer(dst_ids=ids, dma_engine_mask=m, remote_sem=sem,
                                              srcs=[buf[:, lo:hi]], dsts=[buf[:, lo:hi] for _ in ds])], local_sem=T.sem.sent)
        return _count(m)

    def hand_masks(j):
        c = cores[j]
        out = []
        for p, h in enumerate(helpers(j)):
            b = _bits(topo.mask(c, h))
            b = b[len(b) - 4 * (p + 1):len(b) - 4 * p]
            out.append(sum(1 << x for x in b))
        return out

    r = T.rank_of(core)
    if r is None:
        for j in range(n):
            if dests(j) and core in helpers(j):
                p = helpers(j).index(core)
                ne = 0
                g.wait_ge(T.sem.hink, _count(hand_masks(j)[p]))
                ne += send_piece(j, p + 1, 0)
                g.wait_ge(T.sem.hinv, _count(hand_masks(j)[p]))
                ne += send_piece(j, p + 1, 1)
                g.wait_ge(T.sem.sent, ne)
        return

    w = T.tables["WID"][r]
    own = T["kv%d" % (r % NSLOT)]
    g.sync.dma_start(own[:, 0:128], T.k[:, :]).then_inc(T.sem.ldk, 16)
    g.scalar.dma_start(own[:, 128:256], T.v[:, :]).then_inc(T.sem.ldv, 16)
    g.sync.dma_start(T.qs[:, 0:w], T.q[:, 0:w]).then_inc(T.sem.ldq, 16)
    g.vector.memset(T.zero[:, 0:w], 0.0).then_inc(T.sem.zf, 1)

    nsent = 0
    if dests(r):
        for half in (0, 1):
            g.wait_ge(T.sem.ldv if half else T.sem.ldk, 16)
            trs = []
            for p, h in enumerate(helpers(r)):
                lo, hi = piece(p + 1, half)
                rid, pid = topo.addr(h, core)
                m = hand_masks(r)[p]
                trs.append(RemoteDMATransfer(dst_ids=[DstId(rid=rid, pnc=pid)], dma_engine_mask=m,
                                             remote_sem=T.sem.hinv if half else T.sem.hink,
                                             srcs=[own[:, lo:hi]], dsts=[own[:, lo:hi]]))
                nsent += _count(m)
            g.remote_dma_fused(trs, local_sem=T.sem.sent)
            nsent += send_piece(r, 0, half)

    blocks = [r] + list(range(r - 1, max(0, r - WB) - 1, -1))
    last = len(blocks) - 1

    def arrivals(j):
        return sum(_count(off_mask(c, dests(j))) for c in [cores[j]] + helpers(j))

    def s_mm(j):
        i = j % NSLOT
        if j == r:
            g.tensor.wait_ge(T.sem.ldk, 16)
            g.tensor.wait_ge(T.sem.ldq, 16)
        else:
            g.tensor.wait_ge(T.sem["ak%d" % i], arrivals(j))
        g.tensor.matmul(T["pS%d" % i][:, 0:w], T["kv%d" % i][:, 0:128], T.qs[:, 0:w], start=True, stop=True) \
            .then_inc(T.sem["sS%d" % i], 1)

    def o_mm(pos):
        j = blocks[pos]
        i = j % NSLOT
        g.tensor.wait_ge(T.sem["sR%d" % i], 1)
        if j == r:
            g.tensor.wait_ge(T.sem.ldv, 16)
        else:
            g.tensor.wait_ge(T.sem["av%d" % i], arrivals(j))
        mm = g.tensor.matmul(T.pO[:, 0:w], T["kv%d" % i][:, 128:256], T["s%d" % i][:, 0:w], start=(pos == 0), stop=(pos == last))
        if pos == last:
            mm.then_inc(T.sem.sO, 1)

    s_mm(blocks[0])
    o_mm(0)
    for pos in range(1, last + 1):
        s_mm(blocks[pos])
    for pos in range(1, last + 1):
        o_mm(pos)

    g.vector.wait_ge(T.sem.zf, 1)
    for j in blocks:
        i = j % NSLOT
        g.vector.wait_ge(T.sem["sS%d" % i], 1)
        g.vector.tensor_tensor(T["s%d" % i][:, 0:w], T["pS%d" % i][:, 0:w], T.zero[:, 0:w], AluOpType.max) \
            .then_inc(T.sem["sR%d" % i], 1)
    g.vector.wait_ge(T.sem.sO, 1)
    g.vector.tensor_copy(T.ysb[:, 0:w], T.pO[:, 0:w]).then_inc(T.sem.sY, 1)

    g.sync.wait_ge(T.sem.sY, 1)
    g.sync.dma_start(T.y[:, 0:w], T.ysb[:, 0:w]).then_inc(T.sem.st, 16)
    g.sync.wait_ge(T.sem.st, 16)
    if nsent:
        g.wait_ge(T.sem.sent, nsent)
